import numpy as np
import ml_dtypes


def mxq(x, axis, fmt="e4m3"):
    dtype, down = {"e4m3": (ml_dtypes.float8_e4m3fn, 7), "e5m2": (ml_dtypes.float8_e5m2, 14)}[fmt]
    v = np.moveaxis(np.asarray(x, np.float32).astype(ml_dtypes.bfloat16).astype(np.float64), axis, -1)
    blocks = v.reshape(v.shape[:-1] + (-1, 32))
    amax = np.abs(blocks).max(-1, keepdims=True)
    byte = np.maximum(np.where(amax > 0, np.frexp(amax)[1] - 1 + 127, 0) - down, 1)
    scale = np.exp2(byte - 127.0)
    codes = (blocks / scale).astype(np.float32).astype(dtype).astype(np.float64)
    return np.moveaxis((codes * scale).reshape(v.shape), -1, axis)


WIDE = False


def mx_kscale(k):
    if not WIDE:
        return np.ones(k)
    levels = np.array([10, -10, 5, -5, 0])
    if k % 512:
        return np.exp2(np.random.permutation(np.resize(levels, k // 32))).repeat(32)
    a = np.empty((k // 512, 16))
    for p in range(k // 512):
        a[p, :8] = np.random.permutation(np.resize(levels, 8))
        for g in range(8):
            far = levels[np.abs(levels - a[p, g]) >= 10]
            a[p, g + 8] = far[np.random.randint(len(far))]
    return np.exp2(a.ravel()).repeat(32)


def f64(x):
    return np.asarray(x).astype(np.float64)


def striped(idx):
    return np.tile(idx.reshape(-1, 16).T, (8, 1)).astype(np.uint16)


def unstriped(offs):
    return offs[:16].T.reshape(-1).astype(np.int64)


def gelu(v):
    return 0.5 * v * (1.0 + np.tanh(np.sqrt(2.0 / np.pi) * (v + 0.044715 * v**3)))


K, T, D, S, V, N = 512, 4096, 4, 1536, 384, 128


def setup_inputs():
    n = np.random.standard_normal
    s = mx_kscale(K)[:, None]
    return {
        "xT": (n((K, T)) * s).astype(np.float32),
        "w": (n((D, K, N)) / np.sqrt(D * K) / s[None]).astype(np.float32),
        "b": (0.3 * n((N, 1))).astype(np.float32),
        "offs": striped(np.random.permutation(T)[:S]),
    }


def reference(xT, w, b, offs):
    idx = unstriped(offs)
    xq = mxq(f64(xT)[:, idx], 0, "e4m3")
    wq = mxq(f64(w), 1, "e4m3")
    y = sum(wq[d].T @ xq[:, d * V:(d + 1) * V] for d in range(D))
    y = gelu(y + f64(b))
    return y

@@ -1,0 +1,117 @@
+from contextlib import ExitStack
+
+import concourse.mybir as mybir
+
+K, T, D, S, V, N = 512, 4096, 4, 1536, 384, 128
+FLOPS = 2 * K * S * N
+
+F32 = mybir.dt.float32
+BF16 = mybir.dt.bfloat16
+U32 = mybir.dt.uint32
+U16 = mybir.dt.uint16
+U8 = mybir.dt.uint8
+FP8X4 = mybir.dt.float8_e4m3fn_x4
+GELU = mybir.ActivationFunctionType.Gelu_apprx_tanh
+
+P = 128
+PACK = 4
+SLICE = 512
+BLOCK = 128
+
+CHUNKS = [
+    (0, 0, 2048, 1024),
+    (0, 2048, 2048, 1024),
+    (1, 0, 2048, 1024),
+    (1, 2048, 1024, 512),
+    (1, 3072, 512, 320),
+    (1, 3584, 512, 320),
+]
+
+
+def tile_picked_merge_lin_gelu_sub_e_kernel(tc, xT, w, b, offs, out):
+    nc = tc.nc
+    x_view = xT.rearrange("(p u e) c -> p u e c", u=2, e=2)
+    w_view = w.rearrange("d (p j) m -> d p j m", j=PACK)
+
+    with ExitStack() as ctx:
+        keep = ctx.enter_context(tc.tile_pool(name="keep", bufs=1))
+        psum = ctx.enter_context(tc.psum_pool(name="psum", bufs=1))
+
+        offsets = keep.tile([P, S // 16], U16, name="offsets")
+        bias = keep.tile([P, 1], F32, name="bias")
+        warm = keep.tile([P, 1], F32, name="warm")
+        warm_out = keep.tile([P, 1], F32, name="warm_out")
+        pairs = [keep.tile([P, T * 2], BF16, name=f"pairs{u}", align_bytes=64) for u in range(2)]
+        grouped = [keep.tile([P, SLICE * PACK], BF16, name=f"grouped{s}", align_bytes=64) for s in range(S // SLICE)]
+        codes = [keep.tile([P, SLICE], U32, name=f"codes{s}", align_bytes=64) for s in range(S // SLICE)]
+        scales = [keep.tile([P, SLICE], U8, name=f"scales{s}", align_bytes=64) for s in range(S // SLICE)]
+        w_raw = [keep.tile([P, PACK, N], F32, name=f"w_raw{d}") for d in range(D)]
+        w_grouped = keep.tile([P, D * N * PACK], BF16, name="w_grouped", align_bytes=64)
+        w_codes = keep.tile([P, D * N], U32, name="w_codes", align_bytes=64)
+        w_scales = keep.tile([P, D * N], U8, name="w_scales", align_bytes=64)
+        y = keep.tile([P, V], F32, name="y")
+        banks = [psum.tile([P, BLOCK], F32, name=f"bank{g}") for g in range(V // BLOCK)]
+
+        nc.vector.memset(warm[:], 0.0)
+        nc.scalar.activation(warm_out[:], warm[:], GELU)
+        nc.scalar.dma_start(bias[:], b)
+        raws = []
+        for i, (u, t0, width, by_vector) in enumerate(CHUNKS):
+            raw = keep.tile([P, 2, width], F32, name=f"raw{i}")
+            nc.sync.dma_start(raw[:], x_view[:, u, :, t0 : t0 + width])
+            raws.append(raw)
+            if i == 0:
+                nc.sync.dma_start(offsets[:], offs)
+        for d in range(D):
+            nc.sync.dma_start(w_raw[d][:], w_view[d])
+
+        def round_chunk(i):
+            u, t0, width, by_vector = CHUNKS[i]
+            dst = pairs[u][:].rearrange("p (c e) -> p c e", e=2)
+            src = raws[i][:].rearrange("p e c -> p c e")
+            nc.scalar.copy(dst[:, t0 + by_vector : t0 + width, :], src[:, by_vector:width, :])
+            nc.vector.tensor_copy(dst[:, t0 : t0 + by_vector, :], src[:, 0:by_vector, :])
+
+        def gather(u, s):
+            words = grouped[s][:].bitcast(U32).rearrange("p (c u) -> p c u", u=2)
+            lists = offsets[:, s * SLICE // 16 : (s + 1) * SLICE // 16]
+            nc.vector.tensor_copy(words[:, :, u], pairs[u][:].bitcast(U32).indirect(lists))
+
+        def quantize(s):
+            nc.vector.quantize_mx(out=codes[s][:].bitcast(FP8X4), scales=scales[s][:], in_=grouped[s][:])
+
+        def multiply(d, g):
+            s, c = divmod((d * V + g * BLOCK), SLICE)
+            nc.tensor.matmul_mx(
+                out=banks[g][:],
+                lhsT=w_codes[:, d * N : (d + 1) * N].bitcast(FP8X4),
+                lhsT_scale=w_scales[:, d * N : (d + 1) * N],
+                rhs=codes[s][:, c : c + BLOCK].bitcast(FP8X4),
+                rhs_scale=scales[s][:, c : c + BLOCK],
+                start=(d == 0),
+                stop=(d == D - 1),
+            )
+
+        round_chunk(0)
+        round_chunk(1)
+        for s in range(S // SLICE):
+            gather(0, s)
+        for i in range(2, len(CHUNKS)):
+            round_chunk(i)
+        w_dst = w_grouped[:].rearrange("p (d m j) -> p d m j", d=D, j=PACK)
+        for d in range(D):
+            nc.scalar.copy(w_dst[:, d], w_raw[d][:].rearrange("p j m -> p m j"))
+        gather(1, 0)
+        gather(1, 1)
+        quantize(0)
+        gather(1, 2)
+        quantize(1)
+        nc.vector.quantize_mx(out=w_codes[:].bitcast(FP8X4), scales=w_scales[:], in_=w_grouped[:])
+        quantize(2)
+        for d in range(D):
+            for g in range(V // BLOCK):
+                multiply(d, g)
+        for g in range(V // BLOCK):
+            cols = slice(g * BLOCK, (g + 1) * BLOCK)
+            nc.scalar.activation(y[:, cols], banks[g][:], GELU, bias=bias[:])
+        nc.sync.dma_start(out, y[:])

@@ -11,6 +11,8 @@ U32 = mybir.dt.uint32
 U16 = mybir.dt.uint16
 U8 = mybir.dt.uint8
 FP8X4 = mybir.dt.float8_e4m3fn_x4
+MULT = mybir.AluOpType.mult
+ADD = mybir.AluOpType.add
 GELU = mybir.ActivationFunctionType.Gelu_apprx_tanh
 
 P = 128
@@ -21,7 +23,7 @@ BLOCK = 128
 CHUNKS = [
     (0, 0, 2048, 1024),
     (0, 2048, 2048, 1024),
-    (1, 0, 2048, 1024),
+    (1, 0, 2048, 896),
     (1, 2048, 1024, 512),
     (1, 3072, 512, 320),
     (1, 3584, 512, 320),
@@ -43,10 +45,10 @@ def tile_picked_merge_lin_gelu_sub_e_kernel(tc, xT, w, b, offs, out):
         warm_out = keep.tile([P, 1], F32, name="warm_out")
         pairs = [keep.tile([P, T * 2], BF16, name=f"pairs{u}", align_bytes=64) for u in range(2)]
         grouped = [keep.tile([P, SLICE * PACK], BF16, name=f"grouped{s}", align_bytes=64) for s in range(S // SLICE)]
-        codes = [keep.tile([P, SLICE], U32, name=f"codes{s}", align_bytes=64) for s in range(S // SLICE)]
         scales = [keep.tile([P, SLICE], U8, name=f"scales{s}", align_bytes=64) for s in range(S // SLICE)]
         w_raw = [keep.tile([P, PACK, N], F32, name=f"w_raw{d}") for d in range(D)]
-        w_grouped = keep.tile([P, D * N * PACK], BF16, name="w_grouped", align_bytes=64)
+        late = [keep.tile([P, SLICE], U32, name=f"late{s}", align_bytes=64) for s in range(2)]
+        w_grouped = keep.tile([P, D * N * PACK], BF16, name="w_grouped", tag="shared", align_bytes=64)
         w_codes = keep.tile([P, D * N], U32, name="w_codes", align_bytes=64)
         w_scales = keep.tile([P, D * N], U8, name="w_scales", align_bytes=64)
         y = keep.tile([P, V], F32, name="y")
@@ -54,7 +56,6 @@ def tile_picked_merge_lin_gelu_sub_e_kernel(tc, xT, w, b, offs, out):
 
         nc.vector.memset(warm[:], 0.0)
         nc.scalar.activation(warm_out[:], warm[:], GELU)
-        nc.scalar.dma_start(bias[:], b)
         raws = []
         for i, (u, t0, width, by_vector) in enumerate(CHUNKS):
             raw = keep.tile([P, 2, width], F32, name=f"raw{i}")
@@ -64,6 +65,7 @@ def tile_picked_merge_lin_gelu_sub_e_kernel(tc, xT, w, b, offs, out):
                 nc.sync.dma_start(offsets[:], offs)
         for d in range(D):
             nc.sync.dma_start(w_raw[d][:], w_view[d])
+        nc.sync.dma_start(bias[:], b)
 
         def round_chunk(i):
             u, t0, width, by_vector = CHUNKS[i]
@@ -77,8 +79,22 @@ def tile_picked_merge_lin_gelu_sub_e_kernel(tc, xT, w, b, offs, out):
             lists = offsets[:, s * SLICE // 16 : (s + 1) * SLICE // 16]
             nc.vector.tensor_copy(words[:, :, u], pairs[u][:].bitcast(U32).indirect(lists))
 
-        def quantize(s):
-            nc.vector.quantize_mx(out=codes[s][:].bitcast(FP8X4), scales=scales[s][:], in_=grouped[s][:])
+        def gather_plain(s):
+            lists = offsets[:, s * SLICE // 16 : (s + 1) * SLICE // 16]
+            nc.vector.tensor_copy(late[s][:], pairs[1][:].bitcast(U32).indirect(lists))
+
+        def interleave(s):
+            dst = grouped[s][:].rearrange("p (c u e) -> p c u e", u=2, e=2)
+            nc.scalar.copy(dst[:, :, 1, :], late[s][:].bitcast(BF16).rearrange("p (c e) -> p c e", e=2))
+
+        codes = [keep.tile([P, SLICE], U32, name=f"codes{s}", align_bytes=64) for s in range(2)]
+
+        def quantize(s, c0=0, c1=SLICE):
+            nc.vector.quantize_mx(
+                out=codes[s][:, c0:c1].bitcast(FP8X4),
+                scales=scales[s][:, c0:c1],
+                in_=grouped[s][:, c0 * PACK : c1 * PACK],
+            )
 
         def multiply(d, g):
             s, c = divmod((d * V + g * BLOCK), SLICE)
@@ -100,14 +116,18 @@ def tile_picked_merge_lin_gelu_sub_e_kernel(tc, xT, w, b, offs, out):
             round_chunk(i)
         w_dst = w_grouped[:].rearrange("p (d m j) -> p d m j", d=D, j=PACK)
         for d in range(D):
-            nc.scalar.copy(w_dst[:, d], w_raw[d][:].rearrange("p j m -> p m j"))
-        gather(1, 0)
-        gather(1, 1)
-        quantize(0)
-        gather(1, 2)
-        quantize(1)
+            nc.gpsimd.tensor_scalar(w_dst[:, d], w_raw[d][:].rearrange("p j m -> p m j"), 1.0, 0.0, MULT, ADD)
+        gather_plain(0)
+        interleave(0)
+        gather_plain(1)
+        interleave(1)
         nc.vector.quantize_mx(out=w_codes[:].bitcast(FP8X4), scales=w_scales[:], in_=w_grouped[:])
-        quantize(2)
+        gather(1, 2)
+        quantize(0)
+        quantize(1)
+        codes.append(keep.tile([P, SLICE], U32, name="codes2", tag="shared", align_bytes=64))
+        quantize(2, 0, SLICE // 2)
+        quantize(2, SLICE // 2, SLICE)
         for d in range(D):
             for g in range(V // BLOCK):
                 multiply(d, g)

@@ -21,11 +21,9 @@ SLICE = 512
 BLOCK = 128
 
 CHUNKS = [
-    (0, 0, 2048, 1024),
-    (0, 2048, 2048, 1024),
-    (1, 0, 2048, 896),
-    (1, 2048, 1024, 512),
-    (1, 3072, 512, 320),
+    (0, 0, 4096, 2720),
+    (1, 0, 2560, 1664),
+    (1, 2560, 1024, 672),
     (1, 3584, 512, 320),
 ]
 
@@ -47,7 +45,7 @@ def tile_picked_merge_lin_gelu_sub_e_kernel(tc, xT, w, b, offs, out):
         grouped = [keep.tile([P, SLICE * PACK], BF16, name=f"grouped{s}", align_bytes=64) for s in range(S // SLICE)]
         scales = [keep.tile([P, SLICE], U8, name=f"scales{s}", align_bytes=64) for s in range(S // SLICE)]
         w_raw = [keep.tile([P, PACK, N], F32, name=f"w_raw{d}") for d in range(D)]
-        late = [keep.tile([P, SLICE], U32, name=f"late{s}", align_bytes=64) for s in range(2)]
+        picked = [keep.tile([P, 2, SLICE], U32, name=f"picked{s}", align_bytes=64) for s in range(S // SLICE)]
         w_grouped = keep.tile([P, D * N * PACK], BF16, name="w_grouped", tag="shared", align_bytes=64)
         w_codes = keep.tile([P, D * N], U32, name="w_codes", align_bytes=64)
         w_scales = keep.tile([P, D * N], U8, name="w_scales", align_bytes=64)
@@ -75,57 +73,58 @@ def tile_picked_merge_lin_gelu_sub_e_kernel(tc, xT, w, b, offs, out):
             nc.vector.tensor_copy(dst[:, t0 : t0 + by_vector, :], src[:, 0:by_vector, :])
 
         def gather(u, s):
-            words = grouped[s][:].bitcast(U32).rearrange("p (c u) -> p c u", u=2)
             lists = offsets[:, s * SLICE // 16 : (s + 1) * SLICE // 16]
-            nc.vector.tensor_copy(words[:, :, u], pairs[u][:].bitcast(U32).indirect(lists))
-
-        def gather_plain(s):
-            lists = offsets[:, s * SLICE // 16 : (s + 1) * SLICE // 16]
-            nc.vector.tensor_copy(late[s][:], pairs[1][:].bitcast(U32).indirect(lists))
+            nc.vector.tensor_copy(picked[s][:, u, :], pairs[u][:].bitcast(U32).indirect(lists))
 
         def interleave(s):
-            dst = grouped[s][:].rearrange("p (c u e) -> p c u e", u=2, e=2)
-            nc.scalar.copy(dst[:, :, 1, :], late[s][:].bitcast(BF16).rearrange("p (c e) -> p c e", e=2))
+            dst = grouped[s][:].bitcast(F32).rearrange("p (c u) -> p c u", u=2)
+            nc.scalar.copy(dst, picked[s][:].bitcast(F32).rearrange("p u c -> p c u"))
 
-        codes = [keep.tile([P, SLICE], U32, name=f"codes{s}", align_bytes=64) for s in range(2)]
+        early_codes = keep.tile([P, SLICE], U32, name="early_codes", align_bytes=64)
+
+        def code_columns(c0, c1):
+            if c1 <= SLICE:
+                return early_codes[:, c0:c1]
+            return late_codes[:, c0 - SLICE : c1 - SLICE]
 
         def quantize(s, c0=0, c1=SLICE):
             nc.vector.quantize_mx(
-                out=codes[s][:, c0:c1].bitcast(FP8X4),
+                out=code_columns(s * SLICE + c0, s * SLICE + c1).bitcast(FP8X4),
                 scales=scales[s][:, c0:c1],
                 in_=grouped[s][:, c0 * PACK : c1 * PACK],
             )
 
         def multiply(d, g):
-            s, c = divmod((d * V + g * BLOCK), SLICE)
+            j = d * V + g * BLOCK
+            s, c = divmod(j, SLICE)
             nc.tensor.matmul_mx(
                 out=banks[g][:],
                 lhsT=w_codes[:, d * N : (d + 1) * N].bitcast(FP8X4),
                 lhsT_scale=w_scales[:, d * N : (d + 1) * N],
-                rhs=codes[s][:, c : c + BLOCK].bitcast(FP8X4),
+                rhs=code_columns(j, j + BLOCK).bitcast(FP8X4),
                 rhs_scale=scales[s][:, c : c + BLOCK],
                 start=(d == 0),
                 stop=(d == D - 1),
             )
 
         round_chunk(0)
-        round_chunk(1)
         for s in range(S // SLICE):
             gather(0, s)
-        for i in range(2, len(CHUNKS)):
+        for i in range(1, len(CHUNKS)):
             round_chunk(i)
         w_dst = w_grouped[:].rearrange("p (d m j) -> p d m j", d=D, j=PACK)
         for d in range(D):
             nc.gpsimd.tensor_scalar(w_dst[:, d], w_raw[d][:].rearrange("p j m -> p m j"), 1.0, 0.0, MULT, ADD)
-        gather_plain(0)
+        gather(1, 0)
         interleave(0)
-        gather_plain(1)
+        gather(1, 1)
         interleave(1)
-        nc.vector.quantize_mx(out=w_codes[:].bitcast(FP8X4), scales=w_scales[:], in_=w_grouped[:])
         gather(1, 2)
+        interleave(2)
         quantize(0)
+        nc.vector.quantize_mx(out=w_codes[:].bitcast(FP8X4), scales=w_scales[:], in_=w_grouped[:])
+        late_codes = keep.tile([P, 2 * SLICE], U32, name="late_codes", tag="shared", align_bytes=64)
         quantize(1)
-        codes.append(keep.tile([P, SLICE], U32, name="codes2", tag="shared", align_bytes=64))
         quantize(2, 0, SLICE // 2)
         quantize(2, SLICE // 2, SLICE)
         for d in range(D):

from contextlib import ExitStack

import concourse.mybir as mybir

K, T, D, S, V, N = 512, 4096, 4, 1536, 384, 128
FLOPS = 2 * K * S * N

F32 = mybir.dt.float32
BF16 = mybir.dt.bfloat16
U32 = mybir.dt.uint32
U16 = mybir.dt.uint16
U8 = mybir.dt.uint8
FP8X4 = mybir.dt.float8_e4m3fn_x4
MULT = mybir.AluOpType.mult
ADD = mybir.AluOpType.add
GELU = mybir.ActivationFunctionType.Gelu_apprx_tanh

P = 128
PACK = 4
SLICE = 512
BLOCK = 128

CHUNKS = [
    (0, 0, 4096, 2720),
    (1, 0, 2560, 1664),
    (1, 2560, 1024, 672),
    (1, 3584, 512, 320),
]


def tile_picked_merge_lin_gelu_sub_e_kernel(tc, xT, w, b, offs, out):
    nc = tc.nc
    x_view = xT.rearrange("(p u e) c -> p u e c", u=2, e=2)
    w_view = w.rearrange("d (p j) m -> d p j m", j=PACK)

    with ExitStack() as ctx:
        keep = ctx.enter_context(tc.tile_pool(name="keep", bufs=1))
        psum = ctx.enter_context(tc.psum_pool(name="psum", bufs=1))

        offsets = keep.tile([P, S // 16], U16, name="offsets")
        bias = keep.tile([P, 1], F32, name="bias")
        warm = keep.tile([P, 1], F32, name="warm")
        warm_out = keep.tile([P, 1], F32, name="warm_out")
        pairs = [keep.tile([P, T * 2], BF16, name=f"pairs{u}", align_bytes=64) for u in range(2)]
        grouped = [keep.tile([P, SLICE * PACK], BF16, name=f"grouped{s}", align_bytes=64) for s in range(S // SLICE)]
        scales = [keep.tile([P, SLICE], U8, name=f"scales{s}", align_bytes=64) for s in range(S // SLICE)]
        w_raw = [keep.tile([P, PACK, N], F32, name=f"w_raw{d}") for d in range(D)]
        picked = [keep.tile([P, 2, SLICE], U32, name=f"picked{s}", align_bytes=64) for s in range(S // SLICE)]
        w_grouped = keep.tile([P, D * N * PACK], BF16, name="w_grouped", tag="shared", align_bytes=64)
        w_codes = keep.tile([P, D * N], U32, name="w_codes", align_bytes=64)
        w_scales = keep.tile([P, D * N], U8, name="w_scales", align_bytes=64)
        y = keep.tile([P, V], F32, name="y")
        banks = [psum.tile([P, BLOCK], F32, name=f"bank{g}") for g in range(V // BLOCK)]

        nc.vector.memset(warm[:], 0.0)
        nc.scalar.activation(warm_out[:], warm[:], GELU)
        raws = []
        for i, (u, t0, width, by_vector) in enumerate(CHUNKS):
            raw = keep.tile([P, 2, width], F32, name=f"raw{i}")
            nc.sync.dma_start(raw[:], x_view[:, u, :, t0 : t0 + width])
            raws.append(raw)
            if i == 0:
                nc.sync.dma_start(offsets[:], offs)
        for d in range(D):
            nc.sync.dma_start(w_raw[d][:], w_view[d])
        nc.sync.dma_start(bias[:], b)

        def round_chunk(i):
            u, t0, width, by_vector = CHUNKS[i]
            dst = pairs[u][:].rearrange("p (c e) -> p c e", e=2)
            src = raws[i][:].rearrange("p e c -> p c e")
            nc.scalar.copy(dst[:, t0 + by_vector : t0 + width, :], src[:, by_vector:width, :])
            nc.vector.tensor_copy(dst[:, t0 : t0 + by_vector, :], src[:, 0:by_vector, :])

        def gather(u, s):
            lists = offsets[:, s * SLICE // 16 : (s + 1) * SLICE // 16]
            nc.vector.tensor_copy(picked[s][:, u, :], pairs[u][:].bitcast(U32).indirect(lists))

        def interleave(s):
            dst = grouped[s][:].bitcast(F32).rearrange("p (c u) -> p c u", u=2)
            nc.scalar.copy(dst, picked[s][:].bitcast(F32).rearrange("p u c -> p c u"))

        early_codes = keep.tile([P, SLICE], U32, name="early_codes", align_bytes=64)

        def code_columns(c0, c1):
            if c1 <= SLICE:
                return early_codes[:, c0:c1]
            return late_codes[:, c0 - SLICE : c1 - SLICE]

        def quantize(s, c0=0, c1=SLICE):
            nc.vector.quantize_mx(
                out=code_columns(s * SLICE + c0, s * SLICE + c1).bitcast(FP8X4),
                scales=scales[s][:, c0:c1],
                in_=grouped[s][:, c0 * PACK : c1 * PACK],
            )

        def multiply(d, g):
            j = d * V + g * BLOCK
            s, c = divmod(j, SLICE)
            nc.tensor.matmul_mx(
                out=banks[g][:],
                lhsT=w_codes[:, d * N : (d + 1) * N].bitcast(FP8X4),
                lhsT_scale=w_scales[:, d * N : (d + 1) * N],
                rhs=code_columns(j, j + BLOCK).bitcast(FP8X4),
                rhs_scale=scales[s][:, c : c + BLOCK],
                start=(d == 0),
                stop=(d == D - 1),
            )

        round_chunk(0)
        for s in range(S // SLICE):
            gather(0, s)
        for i in range(1, len(CHUNKS)):
            round_chunk(i)
        w_dst = w_grouped[:].rearrange("p (d m j) -> p d m j", d=D, j=PACK)
        for d in range(D):
            nc.gpsimd.tensor_scalar(w_dst[:, d], w_raw[d][:].rearrange("p j m -> p m j"), 1.0, 0.0, MULT, ADD)
        gather(1, 0)
        interleave(0)
        gather(1, 1)
        interleave(1)
        gather(1, 2)
        interleave(2)
        quantize(0)
        nc.vector.quantize_mx(out=w_codes[:].bitcast(FP8X4), scales=w_scales[:], in_=w_grouped[:])
        late_codes = keep.tile([P, 2 * SLICE], U32, name="late_codes", tag="shared", align_bytes=64)
        quantize(1)
        quantize(2, 0, SLICE // 2)
        quantize(2, SLICE // 2, SLICE)
        for d in range(D):
            for g in range(V // BLOCK):
                multiply(d, g)
        for g in range(V // BLOCK):
            cols = slice(g * BLOCK, (g + 1) * BLOCK)
            nc.scalar.activation(y[:, cols], banks[g][:], GELU, bias=bias[:])
        nc.sync.dma_start(out, y[:])
